import numpy as np
import ml_dtypes


def mxq(x, axis, fmt="e4m3"):
    dtype, down = {"e4m3": (ml_dtypes.float8_e4m3fn, 7), "e5m2": (ml_dtypes.float8_e5m2, 14)}[fmt]
    v = np.moveaxis(np.asarray(x, np.float32).astype(ml_dtypes.bfloat16).astype(np.float64), axis, -1)
    blocks = v.reshape(v.shape[:-1] + (-1, 32))
    amax = np.abs(blocks).max(-1, keepdims=True)
    byte = np.maximum(np.where(amax > 0, np.frexp(amax)[1] - 1 + 127, 0) - down, 1)
    scale = np.exp2(byte - 127.0)
    codes = (blocks / scale).astype(np.float32).astype(dtype).astype(np.float64)
    return np.moveaxis((codes * scale).reshape(v.shape), -1, axis)


WIDE = False


def mx_kscale(k):
    if not WIDE:
        return np.ones(k)
    levels = np.array([10, -10, 5, -5, 0])
    if k % 512:
        return np.exp2(np.random.permutation(np.resize(levels, k // 32))).repeat(32)
    a = np.empty((k // 512, 16))
    for p in range(k // 512):
        a[p, :8] = np.random.permutation(np.resize(levels, 8))
        for g in range(8):
            far = levels[np.abs(levels - a[p, g]) >= 10]
            a[p, g + 8] = far[np.random.randint(len(far))]
    return np.exp2(a.ravel()).repeat(32)


def f64(x):
    return np.asarray(x).astype(np.float64)


def striped(idx):
    return np.tile(idx.reshape(-1, 16).T, (8, 1)).astype(np.uint16)


def unstriped(offs):
    return offs[:16].T.reshape(-1).astype(np.int64)


def pack_weight(w):
    k, n = w.shape
    w = f64(np.asarray(w, np.float32).astype(ml_dtypes.bfloat16)).reshape(k // 32, 32, n)
    amax = np.abs(w).max(1)
    byte = np.clip(np.where(amax > 0, np.frexp(amax)[1] - 1 + 127 - 7, 1), 1, 254)
    scaled = (w * np.exp2(127.0 - byte)[:, None, :]).reshape(k, n).astype(np.float32)
    words = np.ascontiguousarray(scaled.reshape(k // 512, 128, 4, n).transpose(0, 1, 3, 2)).astype(ml_dtypes.float8_e4m3fn).view(np.uint8)
    return words, np.ascontiguousarray(byte.astype(np.uint8).reshape(k // 512, 16, n))


def unpack_weight(words, scales):
    g, p, n, _ = words.shape
    vals = np.ascontiguousarray(words).view(ml_dtypes.float8_e4m3fn).astype(np.float64) * np.repeat(np.exp2(scales.astype(np.float64) - 127.0), 8, axis=1)[..., None]
    return vals.transpose(0, 1, 3, 2).reshape(g * 512, n)


def sigmoid(v):
    return 1.0 / (1.0 + np.exp(-np.maximum(v, -700.0)))


K, T, S, V = 512, 2048, 512, 256


def setup_inputs():
    n = np.random.standard_normal
    s = mx_kscale(K)[:, None]
    packed_xT = pack_weight(n((K, T)) * s)
    packed_eT = pack_weight(n((K, T)) * s)
    return {
        "x_words": packed_xT[0],
        "x_scales": packed_xT[1],
        "hT": (n((K, V)) / np.sqrt(K) / s).astype(np.float32),
        "e_words": packed_eT[0],
        "e_scales": packed_eT[1],
        "gT": (n((K, V)) / np.sqrt(K) / s).astype(np.float32),
        "offs": striped(np.random.permutation(T)[:S]),
    }


def reference(x_words, x_scales, hT, e_words, e_scales, gT, offs):
    hTq = mxq(f64(hT), 0, "e4m3")
    xq = unpack_weight(x_words, x_scales)[:, unstriped(offs)]
    y = 1.4 * (hTq.T @ xq)
    ea = np.exp(y)
    sa = np.log(ea.sum(axis=1, keepdims=True))
    la = y - sa
    top = la.max(axis=1, keepdims=True)
    ok = sigmoid(4.0 * (la - top + 2.3))
    gTq = mxq(f64(gT), 0, "e4m3")
    e_offs = unpack_weight(e_words, e_scales)[:, unstriped(offs)]
    z = gTq.T @ e_offs
    eb = np.exp(z)
    sb = np.log(eb.sum(axis=1, keepdims=True))
    lb = z - sb
    ct = 1.5 * la - (0.5 * lb)
    od = ok * ct
    mo = od.mean(axis=1, keepdims=True)
    return ok * (ct - (2.0 * mo))

@@ -1,0 +1,168 @@
+from contextlib import ExitStack
+
+import concourse.mybir as mybir
+
+K, T, S, V = 512, 2048, 512, 256
+P = 128
+PACK = 4
+BLOCKS = V // P
+FLOPS = 2 * 2 * K * V * S
+
+F32 = mybir.dt.float32
+BF16 = mybir.dt.bfloat16
+I32 = mybir.dt.int32
+U32 = mybir.dt.uint32
+U16 = mybir.dt.uint16
+U8 = mybir.dt.uint8
+FP8X4 = mybir.dt.float8_e4m3fn_x4
+ALU = mybir.AluOpType
+ACT = mybir.ActivationFunctionType
+
+
+def tile_picked_ycdec_dev_p_kernel(
+    tc, x_words, x_scales, hT, e_words, e_scales, gT, offs, out
+):
+    nc = tc.nc
+    with ExitStack() as ctx:
+        keep = ctx.enter_context(tc.tile_pool(name="keep", bufs=1))
+        psum = ctx.enter_context(tc.psum_pool(name="psum", bufs=1))
+
+        def sb(name, shape, dtype):
+            return keep.tile(shape, dtype, name=name, align_bytes=64)
+
+        offsets = keep.tile([P, S // 16], U16, name="offsets")
+        xw = sb("xw", [P, T], U32)
+        ew = sb("ew", [P, T], U32)
+        xs = sb("xs", [P, T], U8)
+        es = sb("es", [P, T], U8)
+        h_raw = sb("h_raw", [P, PACK, V], F32)
+        g_raw = sb("g_raw", [P, PACK, V], F32)
+        warm = sb("warm", [P, 1], F32)
+        warm_out = sb("warm_out", [P, 1], F32)
+
+        nc.vector.memset(xs[:].bitcast(I32), 0)
+        nc.gpsimd.memset(es[:].bitcast(I32), 0)
+        nc.vector.memset(warm[:], 0.0)
+
+        def load_scales(eng, tile, dram, q, row):
+            eng.dma_start(tile[32 * q + row : 32 * q + row + 4, :].bitcast(I32), dram[0, 4 * q : 4 * q + 4, :].bitcast(I32))
+
+        def words(dram):
+            return dram[0].rearrange("p n t -> p (n t)").bitcast(I32)
+
+        nc.sync.dma_start(offsets[:], offs)
+        for q in range(3):
+            load_scales(nc.scalar, xs, x_scales, q, 0)
+        load_scales(nc.gpsimd, xs, x_scales, 3, 0)
+        for q in range(4):
+            load_scales(nc.gpsimd, es, e_scales, q, 4)
+        nc.sync.dma_start(h_raw[:], hT.rearrange("(p j) w -> p j w", j=PACK))
+        nc.sync.dma_start(xw[:].bitcast(I32), words(x_words))
+        nc.sync.dma_start(g_raw[:], gT.rearrange("(p j) w -> p j w", j=PACK))
+        nc.sync.dma_start(ew[:].bitcast(I32), words(e_words))
+
+        nc.scalar.activation(warm_out[:], warm[:], ACT.Exp)
+
+        def gather(name, table, dtype):
+            picked = sb(name, [P, S], dtype)
+            nc.vector.tensor_copy(picked[:], table[:].indirect(offsets[:]))
+            return picked
+
+        def cast(name, raw):
+            grouped = sb(name, [P, V, PACK], BF16)
+            nc.scalar.copy(
+                grouped[:].rearrange("p (c i) t -> p c t i", i=4),
+                raw[:].rearrange("p t (c i) -> p c t i", i=4),
+            )
+            return grouped
+
+        def quantise(name, grouped):
+            codes = sb(name + "_codes", [P, V], U32)
+            scales = sb(name + "_scales", [P, V], U8)
+            nc.vector.quantize_mx(
+                out=codes[:].bitcast(FP8X4), scales=scales[:], in_=grouped[:].rearrange("p w j -> p (w j)")
+            )
+            return codes, scales
+
+        def product(name, b, codes, scales, picked_words, picked_scales):
+            acc = psum.tile([P, S], F32, name=name)
+            cols = slice(b * P, (b + 1) * P)
+            nc.tensor.matmul_mx(
+                out=acc[:],
+                lhsT=codes[:, cols].bitcast(FP8X4),
+                lhsT_scale=scales[:, cols],
+                rhs=picked_words[:].bitcast(FP8X4),
+                rhs_scale=picked_scales,
+                start=True,
+                stop=True,
+            )
+            return acc
+
+        def stat(name):
+            return sb(name, [P, 1], F32)
+
+        h_bf = cast("h_bf", h_raw)
+        xs_p = gather("xs_p", xs, U8)
+        h_codes, h_scales = quantise("h", h_bf)
+        es_p = gather("es_p", es, U8)
+        xw_p = gather("xw_p", xw, U32)
+        g_bf = cast("g_bf", g_raw)
+
+        blocks = range(BLOCKS)
+        py = [product("py%d" % b, b, h_codes, h_scales, xw_p, xs_p[:]) for b in blocks]
+        yn = [sb("yn%d" % b, [P, S], F32) for b in blocks]
+        ny = [stat("ny%d" % b) for b in blocks]
+        for b in blocks:
+            nc.vector.tensor_scalar(yn[b][:], py[b][:], -1.4, None, ALU.mult, ALU.min, accum_out=ny[b][:])
+        g_codes, g_scales = quantise("g", g_bf)
+        ew_p = gather("ew_p", ew, U32)
+
+        junk = [sb("junk%d" % i, [P, S], F32) for i in range(2 * BLOCKS)]
+        th = [sb("th%d" % b, [P, S], F32) for b in blocks]
+        ok = [sb("ok%d" % b, [P, S], F32) for b in blocks]
+        tb = [stat("tb%d" % b) for b in blocks]
+        sy = [stat("sy%d" % b) for b in blocks]
+        tsum = [stat("tsum%d" % b) for b in blocks]
+        beta = [stat("beta%d" % b) for b in blocks]
+        sy3 = [stat("sy3%d" % b) for b in blocks]
+        isy3 = [stat("isy3%d" % b) for b in blocks]
+        for b in blocks:
+            nc.scalar.activation(tb[b][:], ny[b][:], ACT.Copy, bias=4.6, scale=2.0)
+            nc.scalar.activation(junk[b][:], yn[b][:], ACT.Exp, bias=ny[b][:], scale=-1.0, accum_out=sy[b][:])
+            nc.scalar.activation(th[b][:], yn[b][:], ACT.Tanh, bias=tb[b][:], scale=-2.0, accum_out=tsum[b][:])
+            nc.gpsimd.tensor_scalar(ok[b][:], th[b][:], 0.75, 0.75, ALU.mult, ALU.add)
+            nc.gpsimd.tensor_scalar(sy3[b][:], sy[b][:], sy[b][:], sy[b][:], ALU.mult, ALU.mult)
+        for b in blocks:
+            nc.scalar.activation(beta[b][:], tsum[b][:], ACT.Copy, scale=1.0 / (3 * S))
+
+        pz = [product("pz%d" % b, b, g_codes, g_scales, ew_p, es_p[4:P, :]) for b in blocks]
+        zn = [sb("zn%d" % b, [P, S], F32) for b in blocks]
+        nz = [stat("nz%d" % b) for b in blocks]
+        sz = [stat("sz%d" % b) for b in blocks]
+        for b in blocks:
+            nc.vector.tensor_scalar(zn[b][:], pz[b][:], -1.0, None, ALU.mult, ALU.min, accum_out=nz[b][:])
+            nc.scalar.activation(junk[BLOCKS + b][:], zn[b][:], ACT.Exp, bias=nz[b][:], scale=-1.0, accum_out=sz[b][:])
+        d = [sb("d%d" % b, [P, S], F32) for b in blocks]
+        shift = [stat("shift%d" % b) for b in blocks]
+        for b in blocks:
+            nc.vector.reciprocal(isy3[b][:], sy3[b][:])
+            nc.vector.scalar_tensor_tensor(d[b][:], pz[b][:], -1.0 / 3.0, yn[b][:], ALU.mult, ALU.subtract)
+            nc.vector.scalar_tensor_tensor(shift[b][:], ny[b][:], 3.0, nz[b][:], ALU.mult, ALU.subtract)
+        w = [sb("w%d" % b, [P, S], F32) for b in blocks]
+        wsum = [stat("wsum%d" % b) for b in blocks]
+        for b in blocks:
+            nc.vector.scalar_tensor_tensor(
+                w[b][:], d[b][:], 4.0 / (3 * S), ok[b][:], ALU.mult, ALU.mult, accum_out=wsum[b][:]
+            )
+        lg = [stat("lg%d" % b) for b in blocks]
+        r0 = [stat("r0%d" % b) for b in blocks]
+        r = [stat("r%d" % b) for b in blocks]
+        for b in blocks:
+            nc.scalar.activation(lg[b][:], sz[b][:], ACT.Ln, scale=isy3[b][:])
+            nc.vector.tensor_scalar(r0[b][:], shift[b][:], beta[b][:], wsum[b][:], ALU.mult, ALU.add)
+        for b in blocks:
+            nc.vector.tensor_scalar(r[b][:], lg[b][:], beta[b][:], r0[b][:], ALU.mult, ALU.add)
+        for b in blocks:
+            res = sb("res%d" % b, [P, S], F32)
+            nc.vector.scalar_tensor_tensor(res[:], d[b][:], r[b][:], ok[b][:], ALU.subtract, ALU.mult)
+            nc.sync.dma_start(out[b * P : (b + 1) * P, :], res[:])

@@ -6,7 +6,15 @@ K, T, S, V = 512, 2048, 512, 256
 P = 128
 PACK = 4
 BLOCKS = V // P
+HALVES = 2
+HALF = S // HALVES
 FLOPS = 2 * 2 * K * V * S
+
+DEGREE = 14
+ROW = 16
+GUESS, SECOND, THIRD = DEGREE - 1, DEGREE, DEGREE + 1
+GUESS_SLOPE = 0.6931471805599453 / 2**23
+GUESS_BIAS = 88.0
 
 F32 = mybir.dt.float32
 BF16 = mybir.dt.bfloat16
@@ -23,50 +31,107 @@ def tile_picked_ycdec_dev_p_kernel(
     tc, x_words, x_scales, hT, e_words, e_scales, gT, offs, out
 ):
     nc = tc.nc
+    blocks = range(BLOCKS)
+    half = [slice(i * HALF, (i + 1) * HALF) for i in range(HALVES)]
     with ExitStack() as ctx:
         keep = ctx.enter_context(tc.tile_pool(name="keep", bufs=1))
         psum = ctx.enter_context(tc.psum_pool(name="psum", bufs=1))
 
-        def sb(name, shape, dtype):
-            return keep.tile(shape, dtype, name=name, align_bytes=64)
+        def sb(name, shape, dtype, tag=None):
+            return keep.tile(shape, dtype, name=name, tag=tag or name, align_bytes=64)
 
         offsets = keep.tile([P, S // 16], U16, name="offsets")
-        xw = sb("xw", [P, T], U32)
-        ew = sb("ew", [P, T], U32)
         xs = sb("xs", [P, T], U8)
         es = sb("es", [P, T], U8)
         h_raw = sb("h_raw", [P, PACK, V], F32)
-        g_raw = sb("g_raw", [P, PACK, V], F32)
         warm = sb("warm", [P, 1], F32)
         warm_out = sb("warm_out", [P, 1], F32)
+        series = sb("series", [P, DEGREE - 1], F32)
+        mul_y = sb("mul_y", [P, BLOCKS * ROW], F32)
+        mul_z = sb("mul_z", [P, BLOCKS * ROW], F32)
+        add_y = sb("add_y", [P, BLOCKS * ROW], F32)
+        add_z = sb("add_z", [P, BLOCKS * ROW], F32)
 
         nc.vector.memset(xs[:].bitcast(I32), 0)
+        nc.gpsimd.memset(warm[:], 0.0)
         nc.gpsimd.memset(es[:].bitcast(I32), 0)
-        nc.vector.memset(warm[:], 0.0)
+        guess_bias = sb("guess_bias", [P, 1], F32)
+        nc.gpsimd.memset(guess_bias[:], GUESS_BIAS)
+        for i, k in enumerate(range(DEGREE - 1, 0, -1)):
+            nc.vector.memset(series[:, i : i + 1], float(k if k % 2 else -k))
+        for add in (add_y, add_z):
+            nc.vector.reciprocal(
+                add[:, 0 : GUESS * BLOCKS].rearrange("p (c b) -> p c b", b=BLOCKS),
+                series[:].unsqueeze(2).to_broadcast([P, GUESS, BLOCKS]),
+            )
 
-        def load_scales(eng, tile, dram, q, row):
-            eng.dma_start(tile[32 * q + row : 32 * q + row + 4, :].bitcast(I32), dram[0, 4 * q : 4 * q + 4, :].bitcast(I32))
+        def step(tile, c):
+            return tile[:, c * BLOCKS : (c + 1) * BLOCKS]
+
+        def cell(tile, c, b):
+            return tile[:, c * BLOCKS + b : c * BLOCKS + b + 1]
+
+        nc.vector.memset(step(mul_y, SECOND), -1.0)
+        nc.vector.memset(step(mul_y, THIRD), -3.0)
+        three_s = sb("three_s", [P, BLOCKS], F32)
+        nc.vector.memset(three_s[:], 3.0 * S)
+        nc.vector.reciprocal(step(mul_z, SECOND), three_s[:])
+
+        xw = sb("xw", [P, T], U32)
+
+        def load_scales(eng, tile, dram, row):
+            for q in (0, 2, 1, 3):
+                eng.dma_start(
+                    tile[32 * q + row : 32 * q + row + 4, :].bitcast(I32), dram[0, 4 * q : 4 * q + 4, :].bitcast(I32)
+                )
 
         def words(dram):
             return dram[0].rearrange("p n t -> p (n t)").bitcast(I32)
 
         nc.sync.dma_start(offsets[:], offs)
-        for q in range(3):
-            load_scales(nc.scalar, xs, x_scales, q, 0)
-        load_scales(nc.gpsimd, xs, x_scales, 3, 0)
-        for q in range(4):
-            load_scales(nc.gpsimd, es, e_scales, q, 4)
         nc.sync.dma_start(h_raw[:], hT.rearrange("(p j) w -> p j w", j=PACK))
+        load_scales(nc.sync, xs, x_scales, 0)
+        nc.scalar.activation(warm_out[:], warm[:], ACT.Exp)
+        ew = sb("ew", [P, T], U32)
+        g_raw = sb("g_raw", [P, PACK, V], F32)
         nc.sync.dma_start(xw[:].bitcast(I32), words(x_words))
+        load_scales(nc.sync, es, e_scales, 4)
         nc.sync.dma_start(g_raw[:], gT.rearrange("(p j) w -> p j w", j=PACK))
         nc.sync.dma_start(ew[:].bitcast(I32), words(e_words))
 
-        nc.scalar.activation(warm_out[:], warm[:], ACT.Exp)
+        def log_start(name, totals):
+            inv = sb(name, [P, BLOCKS], F32)
+            nc.scalar.activation(inv[:], totals[:].bitcast(U32), ACT.Exp, bias=guess_bias[:], scale=-GUESS_SLOPE)
+            return inv
+
+        def log_terms(mul, add, totals, inv):
+            nc.scalar.activation(step(add, GUESS), totals[:].bitcast(U32), ACT.Copy, bias=-GUESS_BIAS, scale=GUESS_SLOPE)
+            for b in blocks:
+                nc.scalar.activation(
+                    mul[:, b : DEGREE * BLOCKS : BLOCKS],
+                    inv[:, b : b + 1].to_broadcast([P, DEGREE]),
+                    ACT.Copy,
+                    bias=-1.0,
+                    scale=totals[:, b : b + 1],
+                )
+
+        def fold(states, mul, add, b):
+            nc.vector.tensor_tensor_scan(
+                states[:, b::BLOCKS], mul[:, b::BLOCKS], add[:, b::BLOCKS], -1.0 / DEGREE, ALU.mult, ALU.add
+            )
 
         def gather(name, table, dtype):
             picked = sb(name, [P, S], dtype)
             nc.vector.tensor_copy(picked[:], table[:].indirect(offsets[:]))
             return picked
+
+        def gather_halves(name, table):
+            halves = []
+            for i in range(HALVES):
+                picked = sb("%s%d" % (name, i), [P, HALF], U32)
+                nc.vector.tensor_copy(picked[:], table[:].indirect(offsets[:, i * HALF // 16 : (i + 1) * HALF // 16]))
+                halves.append(picked)
+            return halves
 
         def cast(name, raw):
             grouped = sb(name, [P, V, PACK], BF16)
@@ -76,93 +141,106 @@ def tile_picked_ycdec_dev_p_kernel(
             )
             return grouped
 
-        def quantise(name, grouped):
-            codes = sb(name + "_codes", [P, V], U32)
+        def quantise(name, grouped, tag=None):
+            codes = sb(name + "_codes", [P, V], U32, tag=tag)
             scales = sb(name + "_scales", [P, V], U8)
             nc.vector.quantize_mx(
                 out=codes[:].bitcast(FP8X4), scales=scales[:], in_=grouped[:].rearrange("p w j -> p (w j)")
             )
             return codes, scales
 
-        def product(name, b, codes, scales, picked_words, picked_scales):
-            acc = psum.tile([P, S], F32, name=name)
-            cols = slice(b * P, (b + 1) * P)
-            nc.tensor.matmul_mx(
-                out=acc[:],
-                lhsT=codes[:, cols].bitcast(FP8X4),
-                lhsT_scale=scales[:, cols],
-                rhs=picked_words[:].bitcast(FP8X4),
-                rhs_scale=picked_scales,
-                start=True,
-                stop=True,
-            )
-            return acc
+        def products(acc, codes, scales, picked_words, picked_scales, row):
+            for i in range(HALVES):
+                for b in blocks:
+                    cols = slice(b * P, (b + 1) * P)
+                    nc.tensor.matmul_mx(
+                        out=acc[b][i],
+                        lhsT=codes[:, cols].bitcast(FP8X4),
+                        lhsT_scale=scales[:, cols],
+                        rhs=picked_words[i][:].bitcast(FP8X4),
+                        rhs_scale=picked_scales[row:P, half[i]],
+                        start=True,
+                        stop=True,
+                    )
 
         def stat(name):
             return sb(name, [P, 1], F32)
 
         h_bf = cast("h_bf", h_raw)
         xs_p = gather("xs_p", xs, U8)
-        h_codes, h_scales = quantise("h", h_bf)
+        h_codes, h_scales = quantise("h", h_bf, tag="xs")
+        xw_p = gather_halves("xw_p", xw)
         es_p = gather("es_p", es, U8)
-        xw_p = gather("xw_p", xw, U32)
         g_bf = cast("g_bf", g_raw)
 
-        blocks = range(BLOCKS)
-        py = [product("py%d" % b, b, h_codes, h_scales, xw_p, xs_p[:]) for b in blocks]
-        yn = [sb("yn%d" % b, [P, S], F32) for b in blocks]
-        ny = [stat("ny%d" % b) for b in blocks]
+        py = [psum.tile([P, S], F32, name="py%d" % b) for b in blocks]
+        products([[py[b][:, cols] for cols in half] for b in blocks], h_codes, h_scales, xw_p, xs_p, 0)
+        ny = [cell(add_y, SECOND, b) for b in blocks]
+        yn_both = sb("yn", [P, BLOCKS * S], F32, tag="es")
+        yn = [yn_both[:, b * S : (b + 1) * S] for b in blocks]
         for b in blocks:
-            nc.vector.tensor_scalar(yn[b][:], py[b][:], -1.4, None, ALU.mult, ALU.min, accum_out=ny[b][:])
+            nc.vector.tensor_scalar(yn[b], py[b][:], -1.4, None, ALU.mult, ALU.min, accum_out=ny[b])
         g_codes, g_scales = quantise("g", g_bf)
-        ew_p = gather("ew_p", ew, U32)
+        ew_p = gather_halves("ew_p", ew)
+        pz = [[psum.tile([P, HALF], F32, name="pz%d%d" % (b, i))[:] for i in range(HALVES)] for b in blocks]
+        products(pz, g_codes, g_scales, ew_p, es_p, 4)
 
-        junk = [sb("junk%d" % i, [P, S], F32) for i in range(2 * BLOCKS)]
-        th = [sb("th%d" % b, [P, S], F32) for b in blocks]
-        ok = [sb("ok%d" % b, [P, S], F32) for b in blocks]
-        tb = [stat("tb%d" % b) for b in blocks]
-        sy = [stat("sy%d" % b) for b in blocks]
-        tsum = [stat("tsum%d" % b) for b in blocks]
-        beta = [stat("beta%d" % b) for b in blocks]
-        sy3 = [stat("sy3%d" % b) for b in blocks]
-        isy3 = [stat("isy3%d" % b) for b in blocks]
+        y_scratch = sb("y_scratch", [P, BLOCKS * (S + 1)], F32, tag="g_raw")
+        exp_y = [y_scratch[:, b * S : (b + 1) * S] for b in blocks]
+        tanh_bias = y_scratch[:, BLOCKS * S :]
+        sy = sb("sy", [P, BLOCKS], F32)
+        ok = [sb("ok0", [P, S], F32, tag="ew_p0"), sb("ok1", [P, S], F32)]
         for b in blocks:
-            nc.scalar.activation(tb[b][:], ny[b][:], ACT.Copy, bias=4.6, scale=2.0)
-            nc.scalar.activation(junk[b][:], yn[b][:], ACT.Exp, bias=ny[b][:], scale=-1.0, accum_out=sy[b][:])
-            nc.scalar.activation(th[b][:], yn[b][:], ACT.Tanh, bias=tb[b][:], scale=-2.0, accum_out=tsum[b][:])
-            nc.gpsimd.tensor_scalar(ok[b][:], th[b][:], 0.75, 0.75, ALU.mult, ALU.add)
-            nc.gpsimd.tensor_scalar(sy3[b][:], sy[b][:], sy[b][:], sy[b][:], ALU.mult, ALU.mult)
-        for b in blocks:
-            nc.scalar.activation(beta[b][:], tsum[b][:], ACT.Copy, scale=1.0 / (3 * S))
+            bias = tanh_bias[:, b : b + 1]
+            nc.scalar.activation(bias, ny[b], ACT.Copy, bias=4.6, scale=2.0)
+            nc.scalar.activation(exp_y[b], yn[b], ACT.Exp, bias=ny[b], scale=-1.0, accum_out=sy[:, b : b + 1])
+            th = sb("th%d" % b, [P, S], F32)
+            nc.scalar.activation(th[:], yn[b], ACT.Tanh, bias=bias, scale=-2.0, accum_out=cell(mul_z, THIRD, b))
+            nc.gpsimd.tensor_scalar(ok[b][:], th[:], 0.75, 0.75, ALU.mult, ALU.add)
+        log_terms(mul_y, add_y, sy, log_start("inv_y", sy))
 
-        pz = [product("pz%d" % b, b, g_codes, g_scales, ew_p, es_p[4:P, :]) for b in blocks]
         zn = [sb("zn%d" % b, [P, S], F32) for b in blocks]
-        nz = [stat("nz%d" % b) for b in blocks]
-        sz = [stat("sz%d" % b) for b in blocks]
+        nz = [cell(add_y, THIRD, b) for b in blocks]
+        nz_first = [stat("nz_first%d" % b) for b in blocks]
+        sz = sb("sz", [P, BLOCKS], F32)
+        exp_z = [sb("exp_z0", [P, S], F32, tag="inv_y"), sb("exp_z1", [P, S], F32)]
         for b in blocks:
-            nc.vector.tensor_scalar(zn[b][:], pz[b][:], -1.0, None, ALU.mult, ALU.min, accum_out=nz[b][:])
-            nc.scalar.activation(junk[BLOCKS + b][:], zn[b][:], ACT.Exp, bias=nz[b][:], scale=-1.0, accum_out=sz[b][:])
+            nc.vector.tensor_scalar(
+                zn[b][:, half[0]], pz[b][0], -1.0, None, ALU.mult, ALU.min, accum_out=nz_first[b][:]
+            )
+        for b in blocks:
+            nc.vector.tensor_scalar(
+                zn[b][:, half[1]], pz[b][1], -1.0, nz_first[b][:], ALU.mult, ALU.min, accum_out=nz[b]
+            )
+            nc.scalar.activation(exp_z[b][:], zn[b][:], ACT.Exp, bias=nz[b], scale=-1.0, accum_out=sz[:, b : b + 1])
         d = [sb("d%d" % b, [P, S], F32) for b in blocks]
-        shift = [stat("shift%d" % b) for b in blocks]
+        states_y = sb("states_y", [P, BLOCKS * ROW], F32)
+
+        def contrast(b):
+            for i in range(HALVES):
+                nc.vector.scalar_tensor_tensor(
+                    d[b][:, half[i]], pz[b][i], -1.0 / 3.0, yn[b][:, half[i]], ALU.mult, ALU.subtract
+                )
+
+        contrast(0)
         for b in blocks:
-            nc.vector.reciprocal(isy3[b][:], sy3[b][:])
-            nc.vector.scalar_tensor_tensor(d[b][:], pz[b][:], -1.0 / 3.0, yn[b][:], ALU.mult, ALU.subtract)
-            nc.vector.scalar_tensor_tensor(shift[b][:], ny[b][:], 3.0, nz[b][:], ALU.mult, ALU.subtract)
-        w = [sb("w%d" % b, [P, S], F32) for b in blocks]
-        wsum = [stat("wsum%d" % b) for b in blocks]
+            fold(states_y, mul_y, add_y, b)
+        contrast(1)
+        inv_z = log_start("inv_z", sz)
+        nc.scalar.activation(step(add_z, SECOND), step(states_y, THIRD), ACT.Copy, scale=-1.0 / (3 * S))
+        log_terms(mul_z, add_z, sz, inv_z)
+        w = sb("w", [P, BLOCKS * S], F32, tag="mul_y")
         for b in blocks:
             nc.vector.scalar_tensor_tensor(
-                w[b][:], d[b][:], 4.0 / (3 * S), ok[b][:], ALU.mult, ALU.mult, accum_out=wsum[b][:]
+                w[:, b * S : (b + 1) * S], d[b][:], 4.0 / (3 * S), ok[b][:], ALU.mult, ALU.mult, accum_out=cell(add_z, THIRD, b)
             )
-        lg = [stat("lg%d" % b) for b in blocks]
-        r0 = [stat("r0%d" % b) for b in blocks]
-        r = [stat("r%d" % b) for b in blocks]
+        states_z = sb("states_z", [P, BLOCKS * ROW], F32)
         for b in blocks:
-            nc.scalar.activation(lg[b][:], sz[b][:], ACT.Ln, scale=isy3[b][:])
-            nc.vector.tensor_scalar(r0[b][:], shift[b][:], beta[b][:], wsum[b][:], ALU.mult, ALU.add)
-        for b in blocks:
-            nc.vector.tensor_scalar(r[b][:], lg[b][:], beta[b][:], r0[b][:], ALU.mult, ALU.add)
-        for b in blocks:
-            res = sb("res%d" % b, [P, S], F32)
-            nc.vector.scalar_tensor_tensor(res[:], d[b][:], r[b][:], ok[b][:], ALU.subtract, ALU.mult)
-            nc.sync.dma_start(out[b * P : (b + 1) * P, :], res[:])
+            fold(states_z, mul_z, add_z, b)
+        for b, pieces in enumerate(([slice(0, S)], half)):
+            for cols in pieces:
+                res = sb("res%d_%d" % (b, cols.start), [P, cols.stop - cols.start], F32)
+                nc.vector.scalar_tensor_tensor(
+                    res[:], d[b][:, cols], cell(states_z, THIRD, b), ok[b][:, cols], ALU.subtract, ALU.mult
+                )
+                nc.sync.dma_start(out[b * P : (b + 1) * P, cols], res[:])

from contextlib import ExitStack

import concourse.mybir as mybir

K, T, S, V = 512, 2048, 512, 256
P = 128
PACK = 4
BLOCKS = V // P
HALVES = 2
HALF = S // HALVES
FLOPS = 2 * 2 * K * V * S

DEGREE = 14
ROW = 16
GUESS, SECOND, THIRD = DEGREE - 1, DEGREE, DEGREE + 1
GUESS_SLOPE = 0.6931471805599453 / 2**23
GUESS_BIAS = 88.0

F32 = mybir.dt.float32
BF16 = mybir.dt.bfloat16
I32 = mybir.dt.int32
U32 = mybir.dt.uint32
U16 = mybir.dt.uint16
U8 = mybir.dt.uint8
FP8X4 = mybir.dt.float8_e4m3fn_x4
ALU = mybir.AluOpType
ACT = mybir.ActivationFunctionType


def tile_picked_ycdec_dev_p_kernel(
    tc, x_words, x_scales, hT, e_words, e_scales, gT, offs, out
):
    nc = tc.nc
    blocks = range(BLOCKS)
    half = [slice(i * HALF, (i + 1) * HALF) for i in range(HALVES)]
    with ExitStack() as ctx:
        keep = ctx.enter_context(tc.tile_pool(name="keep", bufs=1))
        psum = ctx.enter_context(tc.psum_pool(name="psum", bufs=1))

        def sb(name, shape, dtype, tag=None):
            return keep.tile(shape, dtype, name=name, tag=tag or name, align_bytes=64)

        offsets = keep.tile([P, S // 16], U16, name="offsets")
        xs = sb("xs", [P, T], U8)
        es = sb("es", [P, T], U8)
        h_raw = sb("h_raw", [P, PACK, V], F32)
        warm = sb("warm", [P, 1], F32)
        warm_out = sb("warm_out", [P, 1], F32)
        series = sb("series", [P, DEGREE - 1], F32)
        mul_y = sb("mul_y", [P, BLOCKS * ROW], F32)
        mul_z = sb("mul_z", [P, BLOCKS * ROW], F32)
        add_y = sb("add_y", [P, BLOCKS * ROW], F32)
        add_z = sb("add_z", [P, BLOCKS * ROW], F32)

        nc.vector.memset(xs[:].bitcast(I32), 0)
        nc.gpsimd.memset(warm[:], 0.0)
        nc.gpsimd.memset(es[:].bitcast(I32), 0)
        guess_bias = sb("guess_bias", [P, 1], F32)
        nc.gpsimd.memset(guess_bias[:], GUESS_BIAS)
        for i, k in enumerate(range(DEGREE - 1, 0, -1)):
            nc.vector.memset(series[:, i : i + 1], float(k if k % 2 else -k))
        for add in (add_y, add_z):
            nc.vector.reciprocal(
                add[:, 0 : GUESS * BLOCKS].rearrange("p (c b) -> p c b", b=BLOCKS),
                series[:].unsqueeze(2).to_broadcast([P, GUESS, BLOCKS]),
            )

        def step(tile, c):
            return tile[:, c * BLOCKS : (c + 1) * BLOCKS]

        def cell(tile, c, b):
            return tile[:, c * BLOCKS + b : c * BLOCKS + b + 1]

        nc.vector.memset(step(mul_y, SECOND), -1.0)
        nc.vector.memset(step(mul_y, THIRD), -3.0)
        three_s = sb("three_s", [P, BLOCKS], F32)
        nc.vector.memset(three_s[:], 3.0 * S)
        nc.vector.reciprocal(step(mul_z, SECOND), three_s[:])

        xw = sb("xw", [P, T], U32)

        def load_scales(eng, tile, dram, row):
            for q in (0, 2, 1, 3):
                eng.dma_start(
                    tile[32 * q + row : 32 * q + row + 4, :].bitcast(I32), dram[0, 4 * q : 4 * q + 4, :].bitcast(I32)
                )

        def words(dram):
            return dram[0].rearrange("p n t -> p (n t)").bitcast(I32)

        nc.sync.dma_start(offsets[:], offs)
        nc.sync.dma_start(h_raw[:], hT.rearrange("(p j) w -> p j w", j=PACK))
        load_scales(nc.sync, xs, x_scales, 0)
        nc.scalar.activation(warm_out[:], warm[:], ACT.Exp)
        ew = sb("ew", [P, T], U32)
        g_raw = sb("g_raw", [P, PACK, V], F32)
        nc.sync.dma_start(xw[:].bitcast(I32), words(x_words))
        load_scales(nc.sync, es, e_scales, 4)
        nc.sync.dma_start(g_raw[:], gT.rearrange("(p j) w -> p j w", j=PACK))
        nc.sync.dma_start(ew[:].bitcast(I32), words(e_words))

        def log_start(name, totals):
            inv = sb(name, [P, BLOCKS], F32)
            nc.scalar.activation(inv[:], totals[:].bitcast(U32), ACT.Exp, bias=guess_bias[:], scale=-GUESS_SLOPE)
            return inv

        def log_terms(mul, add, totals, inv):
            nc.scalar.activation(step(add, GUESS), totals[:].bitcast(U32), ACT.Copy, bias=-GUESS_BIAS, scale=GUESS_SLOPE)
            for b in blocks:
                nc.scalar.activation(
                    mul[:, b : DEGREE * BLOCKS : BLOCKS],
                    inv[:, b : b + 1].to_broadcast([P, DEGREE]),
                    ACT.Copy,
                    bias=-1.0,
                    scale=totals[:, b : b + 1],
                )

        def fold(states, mul, add, b):
            nc.vector.tensor_tensor_scan(
                states[:, b::BLOCKS], mul[:, b::BLOCKS], add[:, b::BLOCKS], -1.0 / DEGREE, ALU.mult, ALU.add
            )

        def gather(name, table, dtype):
            picked = sb(name, [P, S], dtype)
            nc.vector.tensor_copy(picked[:], table[:].indirect(offsets[:]))
            return picked

        def gather_halves(name, table):
            halves = []
            for i in range(HALVES):
                picked = sb("%s%d" % (name, i), [P, HALF], U32)
                nc.vector.tensor_copy(picked[:], table[:].indirect(offsets[:, i * HALF // 16 : (i + 1) * HALF // 16]))
                halves.append(picked)
            return halves

        def cast(name, raw):
            grouped = sb(name, [P, V, PACK], BF16)
            nc.scalar.copy(
                grouped[:].rearrange("p (c i) t -> p c t i", i=4),
                raw[:].rearrange("p t (c i) -> p c t i", i=4),
            )
            return grouped

        def quantise(name, grouped, tag=None):
            codes = sb(name + "_codes", [P, V], U32, tag=tag)
            scales = sb(name + "_scales", [P, V], U8)
            nc.vector.quantize_mx(
                out=codes[:].bitcast(FP8X4), scales=scales[:], in_=grouped[:].rearrange("p w j -> p (w j)")
            )
            return codes, scales

        def products(acc, codes, scales, picked_words, picked_scales, row):
            for i in range(HALVES):
                for b in blocks:
                    cols = slice(b * P, (b + 1) * P)
                    nc.tensor.matmul_mx(
                        out=acc[b][i],
                        lhsT=codes[:, cols].bitcast(FP8X4),
                        lhsT_scale=scales[:, cols],
                        rhs=picked_words[i][:].bitcast(FP8X4),
                        rhs_scale=picked_scales[row:P, half[i]],
                        start=True,
                        stop=True,
                    )

        def stat(name):
            return sb(name, [P, 1], F32)

        h_bf = cast("h_bf", h_raw)
        xs_p = gather("xs_p", xs, U8)
        h_codes, h_scales = quantise("h", h_bf, tag="xs")
        xw_p = gather_halves("xw_p", xw)
        es_p = gather("es_p", es, U8)
        g_bf = cast("g_bf", g_raw)

        py = [psum.tile([P, S], F32, name="py%d" % b) for b in blocks]
        products([[py[b][:, cols] for cols in half] for b in blocks], h_codes, h_scales, xw_p, xs_p, 0)
        ny = [cell(add_y, SECOND, b) for b in blocks]
        yn_both = sb("yn", [P, BLOCKS * S], F32, tag="es")
        yn = [yn_both[:, b * S : (b + 1) * S] for b in blocks]
        for b in blocks:
            nc.vector.tensor_scalar(yn[b], py[b][:], -1.4, None, ALU.mult, ALU.min, accum_out=ny[b])
        g_codes, g_scales = quantise("g", g_bf)
        ew_p = gather_halves("ew_p", ew)
        pz = [[psum.tile([P, HALF], F32, name="pz%d%d" % (b, i))[:] for i in range(HALVES)] for b in blocks]
        products(pz, g_codes, g_scales, ew_p, es_p, 4)

        y_scratch = sb("y_scratch", [P, BLOCKS * (S + 1)], F32, tag="g_raw")
        exp_y = [y_scratch[:, b * S : (b + 1) * S] for b in blocks]
        tanh_bias = y_scratch[:, BLOCKS * S :]
        sy = sb("sy", [P, BLOCKS], F32)
        ok = [sb("ok0", [P, S], F32, tag="ew_p0"), sb("ok1", [P, S], F32)]
        for b in blocks:
            bias = tanh_bias[:, b : b + 1]
            nc.scalar.activation(bias, ny[b], ACT.Copy, bias=4.6, scale=2.0)
            nc.scalar.activation(exp_y[b], yn[b], ACT.Exp, bias=ny[b], scale=-1.0, accum_out=sy[:, b : b + 1])
            th = sb("th%d" % b, [P, S], F32)
            nc.scalar.activation(th[:], yn[b], ACT.Tanh, bias=bias, scale=-2.0, accum_out=cell(mul_z, THIRD, b))
            nc.gpsimd.tensor_scalar(ok[b][:], th[:], 0.75, 0.75, ALU.mult, ALU.add)
        log_terms(mul_y, add_y, sy, log_start("inv_y", sy))

        zn = [sb("zn%d" % b, [P, S], F32) for b in blocks]
        nz = [cell(add_y, THIRD, b) for b in blocks]
        nz_first = [stat("nz_first%d" % b) for b in blocks]
        sz = sb("sz", [P, BLOCKS], F32)
        exp_z = [sb("exp_z0", [P, S], F32, tag="inv_y"), sb("exp_z1", [P, S], F32)]
        for b in blocks:
            nc.vector.tensor_scalar(
                zn[b][:, half[0]], pz[b][0], -1.0, None, ALU.mult, ALU.min, accum_out=nz_first[b][:]
            )
        for b in blocks:
            nc.vector.tensor_scalar(
                zn[b][:, half[1]], pz[b][1], -1.0, nz_first[b][:], ALU.mult, ALU.min, accum_out=nz[b]
            )
            nc.scalar.activation(exp_z[b][:], zn[b][:], ACT.Exp, bias=nz[b], scale=-1.0, accum_out=sz[:, b : b + 1])
        d = [sb("d%d" % b, [P, S], F32) for b in blocks]
        states_y = sb("states_y", [P, BLOCKS * ROW], F32)

        def contrast(b):
            for i in range(HALVES):
                nc.vector.scalar_tensor_tensor(
                    d[b][:, half[i]], pz[b][i], -1.0 / 3.0, yn[b][:, half[i]], ALU.mult, ALU.subtract
                )

        contrast(0)
        for b in blocks:
            fold(states_y, mul_y, add_y, b)
        contrast(1)
        inv_z = log_start("inv_z", sz)
        nc.scalar.activation(step(add_z, SECOND), step(states_y, THIRD), ACT.Copy, scale=-1.0 / (3 * S))
        log_terms(mul_z, add_z, sz, inv_z)
        w = sb("w", [P, BLOCKS * S], F32, tag="mul_y")
        for b in blocks:
            nc.vector.scalar_tensor_tensor(
                w[:, b * S : (b + 1) * S], d[b][:], 4.0 / (3 * S), ok[b][:], ALU.mult, ALU.mult, accum_out=cell(add_z, THIRD, b)
            )
        states_z = sb("states_z", [P, BLOCKS * ROW], F32)
        for b in blocks:
            fold(states_z, mul_z, add_z, b)
        for b, pieces in enumerate(([slice(0, S)], half)):
            for cols in pieces:
                res = sb("res%d_%d" % (b, cols.start), [P, cols.stop - cols.start], F32)
                nc.vector.scalar_tensor_tensor(
                    res[:], d[b][:, cols], cell(states_z, THIRD, b), ok[b][:, cols], ALU.subtract, ALU.mult
                )
                nc.sync.dma_start(out[b * P : (b + 1) * P, cols], res[:])
